import numpy as np
import ml_dtypes


def mxq(x, axis, fmt="e4m3"):
    dtype, down = {"e4m3": (ml_dtypes.float8_e4m3fn, 7), "e5m2": (ml_dtypes.float8_e5m2, 14)}[fmt]
    v = np.moveaxis(np.asarray(x, np.float32).astype(ml_dtypes.bfloat16).astype(np.float64), axis, -1)
    blocks = v.reshape(v.shape[:-1] + (-1, 32))
    amax = np.abs(blocks).max(-1, keepdims=True)
    byte = np.maximum(np.where(amax > 0, np.frexp(amax)[1] - 1 + 127, 0) - down, 1)
    scale = np.exp2(byte - 127.0)
    codes = (blocks / scale).astype(np.float32).astype(dtype).astype(np.float64)
    return np.moveaxis((codes * scale).reshape(v.shape), -1, axis)


WIDE = False


def mx_kscale(k):
    if not WIDE:
        return np.ones(k)
    levels = np.array([10, -10, 5, -5, 0])
    if k % 512:
        return np.exp2(np.random.permutation(np.resize(levels, k // 32))).repeat(32)
    a = np.empty((k // 512, 16))
    for p in range(k // 512):
        a[p, :8] = np.random.permutation(np.resize(levels, 8))
        for g in range(8):
            far = levels[np.abs(levels - a[p, g]) >= 10]
            a[p, g + 8] = far[np.random.randint(len(far))]
    return np.exp2(a.ravel()).repeat(32)


def f64(x):
    return np.asarray(x).astype(np.float64)


def striped(idx):
    return np.tile(np.asarray(idx).reshape(-1, 16).T, (8, 1)).astype(np.uint16)


def unstriped(offs):
    return offs[:16].T.reshape(-1).astype(np.int64)


E2M1 = np.array([0.0, 0.5, 1.0, 1.5, 2.0, 3.0, 4.0, 6.0, -0.0, -0.5, -1.0, -1.5, -2.0, -3.0, -4.0, -6.0])


def pack_weight(w, fmt):
    k, n = w.shape
    w = f64(np.asarray(w, np.float32).astype(ml_dtypes.bfloat16)).reshape(k // 32, 32, n)
    amax = np.abs(w).max(1)
    if fmt == "e4m3":
        byte = np.frexp(amax)[1] - 1 + 127 - 7
    else:
        mant, ex = np.frexp(amax / 6.0)
        byte = np.where(mant > 0.5, ex, ex - 1) + 127
    byte = np.clip(np.where(amax > 0, byte, 1), 1, 254)
    scaled = (w * np.exp2(127.0 - byte)[:, None, :]).reshape(k, n).astype(np.float32)
    by_word = np.ascontiguousarray(scaled.reshape(k // 512, 128, 4, n).transpose(0, 1, 3, 2))
    if fmt == "e4m3":
        words = by_word.astype(ml_dtypes.float8_e4m3fn).view(np.uint8)
    else:
        c = by_word.astype(ml_dtypes.float4_e2m1fn).view(np.uint8) & 0xF
        words = (c[..., 0::2] | (c[..., 1::2] << 4)).reshape(k // 512, 128, 2 * n)
    return np.ascontiguousarray(words), np.ascontiguousarray(byte.astype(np.uint8).reshape(k // 512, 16, n))


def unpack_weight(words, scales, fmt):
    g, _, n = scales.shape
    words = np.ascontiguousarray(words).reshape(g, 128, n, -1)
    if fmt == "e4m3":
        vals = words.view(ml_dtypes.float8_e4m3fn).astype(np.float64)
    else:
        nib = np.empty((g, 128, n, 4), np.uint8)
        nib[..., 0::2] = words & 0xF
        nib[..., 1::2] = words >> 4
        vals = E2M1[nib]
    vals = vals * np.repeat(np.exp2(scales.astype(np.float64) - 127.0), 8, axis=1)[..., None]
    return vals.transpose(0, 1, 3, 2).reshape(g * 512, n)


def sgn(shape):
    return np.random.uniform(0.5, 2.0, shape) * np.where(np.random.standard_normal(shape) < 0, -1.0, 1.0)


K, Q, T, J, N, U = 512, 128, 1024, 256, 256, 128


def setup_inputs():
    n = np.random.standard_normal
    idx = np.random.permutation(T)[:J]
    idx2 = np.random.permutation(T)[:J]
    idx3 = np.random.permutation(T)[:J]
    idx4 = np.random.permutation(J)[:U]
    idx5 = np.random.permutation(J)[:U]
    fk = mx_kscale(K)
    wp = pack_weight(n((K, N)) * 1 / np.sqrt(K) / fk[:, None], "e2m1")
    return {
        "xt": (0.9 * n((K, T))).astype(np.float32),
        "ga": (sgn((Q, 1)) * fk[::4, None]).astype(np.float32),
        "gb": (sgn((Q, 1)) * fk[::4, None]).astype(np.float32),
        "gc": (sgn((Q, 1)) * fk[::4, None]).astype(np.float32),
        "gd": (sgn((Q, 1)) * fk[::4, None]).astype(np.float32),
        "w_words": wp[0],
        "w_scales": wp[1],
        "so": (np.random.uniform(0.5, 1.6, (N, 1))).astype(np.float32),
        "offs": striped(idx),
        "offs2": striped(idx2),
        "offs3": striped(idx3),
        "offs4": striped(idx4),
        "offs5": striped(idx5),
    }


def reference(xt, ga, gb, gc, gd, w_words, w_scales, so, offs, offs2, offs3, offs4, offs5):
    idx = unstriped(offs)
    idx2 = unstriped(offs2)
    idx3 = unstriped(offs3)
    idx4 = unstriped(offs4)
    idx5 = unstriped(offs5)
    wu = unpack_weight(w_words, w_scales, "e2m1")
    x0 = f64(xt)[0::4]
    x1 = f64(xt)[1::4]
    x2 = f64(xt)[2::4]
    x3 = f64(xt)[3::4]
    v0 = x0[:, idx] * f64(ga)
    v1 = x1[:, idx2] * f64(gb)
    v2 = x2[:, idx3] * f64(gc)
    v3 = x3[:, idx] * f64(gd)
    z = np.stack([v0, v1, v2, v3], axis=1).reshape(K, J)
    zq = mxq(z, 0, "e4m3")
    p = wu.T @ zq
    y = np.abs(p[:, idx4] * f64(so) - p[:, idx5])
    return y

@@ -1,0 +1,129 @@
+from contextlib import ExitStack
+
+import concourse.mybir as mybir
+
+K, T, J, N, U = 512, 1024, 256, 256, 128
+FLOPS = 2 * K * N * J
+
+F32 = mybir.dt.float32
+BF16 = mybir.dt.bfloat16
+I32 = mybir.dt.int32
+U32 = mybir.dt.uint32
+U16 = mybir.dt.uint16
+U8 = mybir.dt.uint8
+FP8X4 = mybir.dt.float8_e4m3fn_x4
+FP4X4 = mybir.dt.float4_e2m1fn_x4
+COPY = mybir.ActivationFunctionType.Copy
+ALU = mybir.AluOpType
+
+P = 128
+BANDS = 4
+GROUP = 16
+HALF = J // 2
+ROW_TILES = N // P
+
+
+def tile_list_fourbands_kernel(tc, xt, ga, gb, gc, gd, w_words, w_scales, so, offs, offs2, offs3, offs4, offs5, out):
+    nc = tc.nc
+    with ExitStack() as ctx:
+        keep = ctx.enter_context(tc.tile_pool(name="keep", bufs=1))
+        psum = ctx.enter_context(tc.psum_pool(name="psum", bufs=1))
+
+        def load_list(src, name):
+            lst = keep.tile(list(src.shape), U16, name=name)
+            nc.sync.dma_start(lst[:], src)
+            return lst
+
+        def load_gain(queue, src, name):
+            gain = keep.tile([P, 1], F32, name=name)
+            queue.dma_start(gain[:], src)
+            return gain
+
+        bands = xt.rearrange("(q g) t -> g q t", g=BANDS)
+
+        def load_band(g):
+            band = keep.tile([P, T], F32, name="band%d" % g)
+            nc.sync.dma_start(band[:], bands[g])
+            return band
+
+        gain_a = load_gain(nc.scalar, ga, "gain_a")
+        gain_d = load_gain(nc.gpsimd, gd, "gain_d")
+        gain_b = load_gain(nc.gpsimd, gb, "gain_b")
+        gain_c = load_gain(nc.gpsimd, gc, "gain_c")
+        weight = keep.tile([P, ROW_TILES, 1], F32)
+        with nc.allow_non_contiguous_dma(reason="one weight a partition"):
+            nc.gpsimd.dma_start(weight[:], so.rearrange("(h p) one -> p h one", p=P))
+        band_a = load_band(0)
+        list_a = load_list(offs, "list_a")
+        band_d = load_band(3)
+        list_b = load_list(offs2, "list_b")
+        band_b = load_band(1)
+        list_c = load_list(offs3, "list_c")
+        band_c = load_band(2)
+        w_codes = keep.tile([P, 2 * N], U8, align_bytes=64)
+        nc.sync.dma_start(w_codes[:].bitcast(I32), w_words[0].bitcast(I32))
+        w_plane = keep.tile([P, N], U8, align_bytes=64)
+        for quad in range(4):
+            nc.sync.dma_start(
+                w_plane[32 * quad : 32 * quad + 4, :].bitcast(I32),
+                w_scales[0, 4 * quad : 4 * quad + 4, :].bitcast(I32),
+            )
+        list_scaled = load_list(offs4, "list_scaled")
+        list_plain = load_list(offs5, "list_plain")
+
+        z = keep.tile([P, BANDS * J], BF16, align_bytes=64)
+
+        def fetch(g, band, lst, gain, j0, j1):
+            nc.scalar.activation(
+                out=z[:, BANDS * j0 + g : BANDS * j1 : BANDS],
+                in_=band[:].indirect(lst[:, j0 // GROUP : j1 // GROUP]),
+                func=COPY,
+                scale=gain[:],
+            )
+
+        fetch(0, band_a, list_a, gain_a, 0, J)
+        fetch(3, band_d, list_a, gain_d, 0, J)
+        fetch(1, band_b, list_b, gain_b, 0, J)
+
+        z_codes = keep.tile([P, J], U32, align_bytes=64)
+        z_plane = keep.tile([P, J], U8, align_bytes=64)
+        for half in range(2):
+            j0, j1 = half * HALF, (half + 1) * HALF
+            fetch(2, band_c, list_c, gain_c, j0, j1)
+            nc.vector.quantize_mx(
+                out=z_codes[:, j0:j1].bitcast(FP8X4),
+                scales=z_plane[:, j0:j1],
+                in_=z[:, BANDS * j0 : BANDS * j1],
+            )
+
+        prod = [keep.tile([P, J], F32, name="prod%d" % h) for h in range(ROW_TILES)]
+        for half in range(2):
+            j0, j1 = half * HALF, (half + 1) * HALF
+            for h in range(ROW_TILES):
+                acc = psum.tile([P, HALF], F32, name="acc%d%d" % (half, h))
+                nc.tensor.matmul_mx(
+                    out=acc[:],
+                    lhsT=w_codes[:, 2 * P * h : 2 * P * (h + 1)].bitcast(FP4X4),
+                    lhsT_scale=w_plane[:, P * h : P * (h + 1)],
+                    rhs=z_codes[:, j0:j1].bitcast(FP8X4),
+                    rhs_scale=z_plane[:, j0:j1],
+                    start=True,
+                    stop=True,
+                )
+                if half == 1:
+                    nc.vector.tensor_copy(out=prod[h][:, j0:j1], in_=acc[:])
+                else:
+                    nc.scalar.copy(out=prod[h][:, j0:j1], in_=acc[:])
+
+        scaled = [keep.tile([P, U], F32, name="scaled%d" % h) for h in range(ROW_TILES)]
+        plain = [keep.tile([P, U], F32, name="plain%d" % h) for h in range(ROW_TILES)]
+        diff = [keep.tile([P, U], F32, name="diff%d" % h) for h in range(ROW_TILES)]
+        size = [keep.tile([P, U], F32, name="size%d" % h) for h in range(ROW_TILES)]
+        for h in range(ROW_TILES):
+            nc.scalar.activation(out=scaled[h][:], in_=prod[h][:].indirect(list_scaled[:]), func=COPY, scale=weight[:, h, :])
+            nc.vector.tensor_copy(out=plain[h][:], in_=prod[h][:].indirect(list_plain[:]))
+        for h in range(ROW_TILES):
+            nc.vector.tensor_tensor(out=diff[h][:], in0=scaled[h][:], in1=plain[h][:], op=ALU.subtract)
+        for h in range(ROW_TILES):
+            nc.vector.scalar_tensor_tensor(out=size[h][:], in0=diff[h][:], scalar=-1.0, in1=diff[h][:], op0=ALU.mult, op1=ALU.max)
+            nc.sync.dma_start(out[P * h : P * (h + 1), :], size[h][:])

@@ -48,6 +48,9 @@ def tile_list_fourbands_kernel(tc, xt, ga, gb, gc, gd, w_words, w_scales, so, of
 
         gain_a = load_gain(nc.scalar, ga, "gain_a")
         gain_d = load_gain(nc.gpsimd, gd, "gain_d")
+        warm = keep.tile([P, 2], F32)
+        nc.vector.memset(warm[:, 0:1], 0.0)
+        nc.scalar.activation(out=warm[:, 1:2], in_=warm[:, 0:1], func=COPY)
         gain_b = load_gain(nc.gpsimd, gb, "gain_b")
         gain_c = load_gain(nc.gpsimd, gc, "gain_c")
         weight = keep.tile([P, ROW_TILES, 1], F32)

@@ -47,20 +47,17 @@ def tile_list_fourbands_kernel(tc, xt, ga, gb, gc, gd, w_words, w_scales, so, of
             return band
 
         gain_a = load_gain(nc.scalar, ga, "gain_a")
-        gain_d = load_gain(nc.gpsimd, gd, "gain_d")
+        gain_d = load_gain(nc.scalar, gd, "gain_d")
+        gain_b = load_gain(nc.scalar, gb, "gain_b")
+        gain_c = load_gain(nc.scalar, gc, "gain_c")
         warm = keep.tile([P, 2], F32)
         nc.vector.memset(warm[:, 0:1], 0.0)
         nc.scalar.activation(out=warm[:, 1:2], in_=warm[:, 0:1], func=COPY)
-        gain_b = load_gain(nc.gpsimd, gb, "gain_b")
-        gain_c = load_gain(nc.gpsimd, gc, "gain_c")
-        weight = keep.tile([P, ROW_TILES, 1], F32)
-        with nc.allow_non_contiguous_dma(reason="one weight a partition"):
-            nc.gpsimd.dma_start(weight[:], so.rearrange("(h p) one -> p h one", p=P))
-        band_a = load_band(0)
         list_a = load_list(offs, "list_a")
+        band_a = load_band(0)
         band_d = load_band(3)
-        list_b = load_list(offs2, "list_b")
         band_b = load_band(1)
+        list_b = load_list(offs2, "list_b")
         list_c = load_list(offs3, "list_c")
         band_c = load_band(2)
         w_codes = keep.tile([P, 2 * N], U8, align_bytes=64)
@@ -73,6 +70,9 @@ def tile_list_fourbands_kernel(tc, xt, ga, gb, gc, gd, w_words, w_scales, so, of
             )
         list_scaled = load_list(offs4, "list_scaled")
         list_plain = load_list(offs5, "list_plain")
+        weight = keep.tile([P, ROW_TILES, 1], F32)
+        with nc.allow_non_contiguous_dma(reason="one weight a partition"):
+            nc.sync.dma_start(weight[:], so.rearrange("(h p) one -> p h one", p=P))
 
         z = keep.tile([P, BANDS * J], BF16, align_bytes=64)
 
@@ -113,7 +113,7 @@ def tile_list_fourbands_kernel(tc, xt, ga, gb, gc, gd, w_words, w_scales, so, of
                     start=True,
                     stop=True,
                 )
-                if half == 1:
+                if h == 0:
                     nc.vector.tensor_copy(out=prod[h][:, j0:j1], in_=acc[:])
                 else:
                     nc.scalar.copy(out=prod[h][:, j0:j1], in_=acc[:])

from contextlib import ExitStack

import concourse.mybir as mybir

K, T, J, N, U = 512, 1024, 256, 256, 128
FLOPS = 2 * K * N * J

F32 = mybir.dt.float32
BF16 = mybir.dt.bfloat16
I32 = mybir.dt.int32
U32 = mybir.dt.uint32
U16 = mybir.dt.uint16
U8 = mybir.dt.uint8
FP8X4 = mybir.dt.float8_e4m3fn_x4
FP4X4 = mybir.dt.float4_e2m1fn_x4
COPY = mybir.ActivationFunctionType.Copy
ALU = mybir.AluOpType

P = 128
BANDS = 4
GROUP = 16
HALF = J // 2
ROW_TILES = N // P


def tile_list_fourbands_kernel(tc, xt, ga, gb, gc, gd, w_words, w_scales, so, offs, offs2, offs3, offs4, offs5, out):
    nc = tc.nc
    with ExitStack() as ctx:
        keep = ctx.enter_context(tc.tile_pool(name="keep", bufs=1))
        psum = ctx.enter_context(tc.psum_pool(name="psum", bufs=1))

        def load_list(src, name):
            lst = keep.tile(list(src.shape), U16, name=name)
            nc.sync.dma_start(lst[:], src)
            return lst

        def load_gain(queue, src, name):
            gain = keep.tile([P, 1], F32, name=name)
            queue.dma_start(gain[:], src)
            return gain

        bands = xt.rearrange("(q g) t -> g q t", g=BANDS)

        def load_band(g):
            band = keep.tile([P, T], F32, name="band%d" % g)
            nc.sync.dma_start(band[:], bands[g])
            return band

        gain_a = load_gain(nc.scalar, ga, "gain_a")
        gain_d = load_gain(nc.scalar, gd, "gain_d")
        gain_b = load_gain(nc.scalar, gb, "gain_b")
        gain_c = load_gain(nc.scalar, gc, "gain_c")
        warm = keep.tile([P, 2], F32)
        nc.vector.memset(warm[:, 0:1], 0.0)
        nc.scalar.activation(out=warm[:, 1:2], in_=warm[:, 0:1], func=COPY)
        list_a = load_list(offs, "list_a")
        band_a = load_band(0)
        band_d = load_band(3)
        band_b = load_band(1)
        list_b = load_list(offs2, "list_b")
        list_c = load_list(offs3, "list_c")
        band_c = load_band(2)
        w_codes = keep.tile([P, 2 * N], U8, align_bytes=64)
        nc.sync.dma_start(w_codes[:].bitcast(I32), w_words[0].bitcast(I32))
        w_plane = keep.tile([P, N], U8, align_bytes=64)
        for quad in range(4):
            nc.sync.dma_start(
                w_plane[32 * quad : 32 * quad + 4, :].bitcast(I32),
                w_scales[0, 4 * quad : 4 * quad + 4, :].bitcast(I32),
            )
        list_scaled = load_list(offs4, "list_scaled")
        list_plain = load_list(offs5, "list_plain")
        weight = keep.tile([P, ROW_TILES, 1], F32)
        with nc.allow_non_contiguous_dma(reason="one weight a partition"):
            nc.sync.dma_start(weight[:], so.rearrange("(h p) one -> p h one", p=P))

        z = keep.tile([P, BANDS * J], BF16, align_bytes=64)

        def fetch(g, band, lst, gain, j0, j1):
            nc.scalar.activation(
                out=z[:, BANDS * j0 + g : BANDS * j1 : BANDS],
                in_=band[:].indirect(lst[:, j0 // GROUP : j1 // GROUP]),
                func=COPY,
                scale=gain[:],
            )

        fetch(0, band_a, list_a, gain_a, 0, J)
        fetch(3, band_d, list_a, gain_d, 0, J)
        fetch(1, band_b, list_b, gain_b, 0, J)

        z_codes = keep.tile([P, J], U32, align_bytes=64)
        z_plane = keep.tile([P, J], U8, align_bytes=64)
        for half in range(2):
            j0, j1 = half * HALF, (half + 1) * HALF
            fetch(2, band_c, list_c, gain_c, j0, j1)
            nc.vector.quantize_mx(
                out=z_codes[:, j0:j1].bitcast(FP8X4),
                scales=z_plane[:, j0:j1],
                in_=z[:, BANDS * j0 : BANDS * j1],
            )

        prod = [keep.tile([P, J], F32, name="prod%d" % h) for h in range(ROW_TILES)]
        for half in range(2):
            j0, j1 = half * HALF, (half + 1) * HALF
            for h in range(ROW_TILES):
                acc = psum.tile([P, HALF], F32, name="acc%d%d" % (half, h))
                nc.tensor.matmul_mx(
                    out=acc[:],
                    lhsT=w_codes[:, 2 * P * h : 2 * P * (h + 1)].bitcast(FP4X4),
                    lhsT_scale=w_plane[:, P * h : P * (h + 1)],
                    rhs=z_codes[:, j0:j1].bitcast(FP8X4),
                    rhs_scale=z_plane[:, j0:j1],
                    start=True,
                    stop=True,
                )
                if h == 0:
                    nc.vector.tensor_copy(out=prod[h][:, j0:j1], in_=acc[:])
                else:
                    nc.scalar.copy(out=prod[h][:, j0:j1], in_=acc[:])

        scaled = [keep.tile([P, U], F32, name="scaled%d" % h) for h in range(ROW_TILES)]
        plain = [keep.tile([P, U], F32, name="plain%d" % h) for h in range(ROW_TILES)]
        diff = [keep.tile([P, U], F32, name="diff%d" % h) for h in range(ROW_TILES)]
        size = [keep.tile([P, U], F32, name="size%d" % h) for h in range(ROW_TILES)]
        for h in range(ROW_TILES):
            nc.scalar.activation(out=scaled[h][:], in_=prod[h][:].indirect(list_scaled[:]), func=COPY, scale=weight[:, h, :])
            nc.vector.tensor_copy(out=plain[h][:], in_=prod[h][:].indirect(list_plain[:]))
        for h in range(ROW_TILES):
            nc.vector.tensor_tensor(out=diff[h][:], in0=scaled[h][:], in1=plain[h][:], op=ALU.subtract)
        for h in range(ROW_TILES):
            nc.vector.scalar_tensor_tensor(out=size[h][:], in0=diff[h][:], scalar=-1.0, in1=diff[h][:], op0=ALU.mult, op1=ALU.max)
            nc.sync.dma_start(out[P * h : P * (h + 1), :], size[h][:])
